import numpy as np
import ml_dtypes


def mxq(x, axis, fmt="e4m3"):
    dtype, down = {"e4m3": (ml_dtypes.float8_e4m3fn, 7), "e5m2": (ml_dtypes.float8_e5m2, 14)}[fmt]
    v = np.moveaxis(np.asarray(x, np.float32).astype(ml_dtypes.bfloat16).astype(np.float64), axis, -1)
    blocks = v.reshape(v.shape[:-1] + (-1, 32))
    amax = np.abs(blocks).max(-1, keepdims=True)
    byte = np.maximum(np.where(amax > 0, np.frexp(amax)[1] - 1 + 127, 0) - down, 1)
    scale = np.exp2(byte - 127.0)
    codes = (blocks / scale).astype(np.float32).astype(dtype).astype(np.float64)
    return np.moveaxis((codes * scale).reshape(v.shape), -1, axis)


WIDE = False


def mx_kscale(k):
    if not WIDE:
        return np.ones(k)
    levels = np.array([10, -10, 5, -5, 0])
    if k % 512:
        return np.exp2(np.random.permutation(np.resize(levels, k // 32))).repeat(32)
    a = np.empty((k // 512, 16))
    for p in range(k // 512):
        a[p, :8] = np.random.permutation(np.resize(levels, 8))
        for g in range(8):
            far = levels[np.abs(levels - a[p, g]) >= 10]
            a[p, g + 8] = far[np.random.randint(len(far))]
    return np.exp2(a.ravel()).repeat(32)


def f64(x):
    return np.asarray(x).astype(np.float64)


def striped(idx):
    return np.tile(np.asarray(idx).reshape(-1, 16).T, (8, 1)).astype(np.uint16)


def unstriped(offs):
    return offs[:16].T.reshape(-1).astype(np.int64)


E2M1 = np.array([0.0, 0.5, 1.0, 1.5, 2.0, 3.0, 4.0, 6.0, -0.0, -0.5, -1.0, -1.5, -2.0, -3.0, -4.0, -6.0])


def pack_weight(w, fmt):
    k, n = w.shape
    w = f64(np.asarray(w, np.float32).astype(ml_dtypes.bfloat16)).reshape(k // 32, 32, n)
    amax = np.abs(w).max(1)
    if fmt == "e4m3":
        byte = np.frexp(amax)[1] - 1 + 127 - 7
    else:
        mant, ex = np.frexp(amax / 6.0)
        byte = np.where(mant > 0.5, ex, ex - 1) + 127
    byte = np.clip(np.where(amax > 0, byte, 1), 1, 254)
    scaled = (w * np.exp2(127.0 - byte)[:, None, :]).reshape(k, n).astype(np.float32)
    by_word = np.ascontiguousarray(scaled.reshape(k // 512, 128, 4, n).transpose(0, 1, 3, 2))
    if fmt == "e4m3":
        words = by_word.astype(ml_dtypes.float8_e4m3fn).view(np.uint8)
    else:
        c = by_word.astype(ml_dtypes.float4_e2m1fn).view(np.uint8) & 0xF
        words = (c[..., 0::2] | (c[..., 1::2] << 4)).reshape(k // 512, 128, 2 * n)
    return np.ascontiguousarray(words), np.ascontiguousarray(byte.astype(np.uint8).reshape(k // 512, 16, n))


def unpack_weight(words, scales, fmt):
    g, _, n = scales.shape
    words = np.ascontiguousarray(words).reshape(g, 128, n, -1)
    if fmt == "e4m3":
        vals = words.view(ml_dtypes.float8_e4m3fn).astype(np.float64)
    else:
        nib = np.empty((g, 128, n, 4), np.uint8)
        nib[..., 0::2] = words & 0xF
        nib[..., 1::2] = words >> 4
        vals = E2M1[nib]
    vals = vals * np.repeat(np.exp2(scales.astype(np.float64) - 127.0), 8, axis=1)[..., None]
    return vals.transpose(0, 1, 3, 2).reshape(g * 512, n)


B, N, T, D, DV, NQ = 1, 512, 1024, 1024, 256, 256


def setup_inputs():
    n = np.random.standard_normal
    idx = np.sort(np.random.permutation(T)[:B * N].reshape(B, N), axis=1).reshape(-1)
    s = mx_kscale(D)[:, None]
    u = np.ones(T)
    u[idx] = mx_kscale(B * N)
    r = np.random.uniform(0.5, 2.0, T)
    qp = [pack_weight(x, "e4m3") for x in n((B, D, NQ)) * s * (1.00 / np.sqrt(D))]
    k = n((D, T)) / s
    v = n((DV, T)) / (u * r)
    kp = pack_weight(k, "e2m1")
    return {
        "q_words": np.stack([x[0] for x in qp]),
        "q_scales": np.stack([x[1] for x in qp]),
        "k_words": np.ascontiguousarray(kp[0].reshape(D // 1024, 2, 128, T, 2).transpose(0, 2, 3, 1, 4)).reshape(D // 1024, 128, T, 4),
        "k_scales": kp[1],
        "vT": v.astype(np.float32),
        "vs": np.tile(u * r, (128, 1)).astype(np.float32),
        "kb": np.tile(n(T), (128, 1)).astype(np.float32),
        "og": n((B, NQ, DV)).astype(np.float32),
        "offs": striped(idx),
    }


def reference(q_words, q_scales, k_words, k_scales, vT, vs, kb, og, offs):
    idx = unstriped(offs)
    k = unpack_weight(k_words.reshape(D // 1024, 128, T, 2, 2).transpose(0, 3, 1, 2, 4).reshape(D // 512, 128, 2 * T), k_scales, "e2m1")
    v = f64(vT)
    pick = lambda x: x[:, idx].reshape(x.shape[0], B, N).transpose(1, 0, 2)
    q = np.stack([unpack_weight(q_words[b], q_scales[b], "e4m3") for b in range(B)])
    score = q.transpose(0, 2, 1) @ pick(k)
    score = score + pick(f64(kb))[:, :1, :]
    p = np.square(np.maximum(score, 0.0))
    total = p.sum(-1, keepdims=True) + 1.0
    w = p * pick(f64(vs))[:, :1, :]
    y = mxq(w, 2, "e4m3") @ mxq(pick(v).transpose(0, 2, 1), 1, "e4m3")
    y = y / total
    y = y / (1.0 + np.exp(-f64(og)))
    return y

from contextlib import ExitStack

import concourse.mybir as mybir
from concourse.masks import make_identity

NQ, N, T, D, DV = 256, 512, 1024, 1024, 256
FLOPS = 2 * NQ * N * D + 2 * NQ * N * DV

F32 = mybir.dt.float32
BF16 = mybir.dt.bfloat16
I32 = mybir.dt.int32
U32 = mybir.dt.uint32
U16 = mybir.dt.uint16
U8 = mybir.dt.uint8
FP8X4 = mybir.dt.float8_e4m3fn_x4
FP4X4 = mybir.dt.float4_e2m1fn_x4
ACT = mybir.ActivationFunctionType
ALU = mybir.AluOpType

P = 128
PLACES = 4
RUN = 8
PASSES = D // 512
HALVES = NQ // P


def tile_attend_rel2_kb_gate_srtq256n512t1024_kernel(
    tc, q_words, q_scales, k_words, k_scales, vT, vs, kb, og, offs, out
):
    nc = tc.nc
    with ExitStack() as ctx:
        sb = ctx.enter_context(tc.tile_pool(name="sb", bufs=1))
        ps = ctx.enter_context(tc.psum_pool(name="ps", bufs=1))

        def dealt(ap):
            return ap.rearrange("p (t g i) -> p g t i", t=PLACES, i=RUN)

        offsets = sb.tile([P, N // 16], U16, name="offsets")
        nc.sync.dma_start(offsets[:], offs)

        ks_pool = sb.tile([P, PASSES * T], U8, name="ks_pool", align_bytes=64)
        kb_pool = sb.tile([P, T], F32, name="kb_pool")
        vs_pool = sb.tile([P, T], F32, name="vs_pool")
        qs = sb.tile([P, PASSES * NQ], U8, name="qs", align_bytes=64)
        warm = sb.tile([P, 8], F32, name="warm", tag="values0")
        nc.gpsimd.memset(warm[:], 0.0)
        nc.gpsimd.memset(qs[:].bitcast(I32), 0)
        nc.vector.memset(kb_pool[:], 0.0)
        nc.vector.memset(ks_pool[:].bitcast(I32), 0)
        nc.vector.memset(vs_pool[:], 0.0)
        warm_out = sb.tile([P, 8], F32, name="warm_out", tag="values1")
        nc.scalar.activation(warm_out[:], warm[:], ACT.Sigmoid)
        ident = sb.tile([P, P], F32, name="ident")
        make_identity(nc, ident[:])

        kw_pool = sb.tile([P, T], I32, name="kw_pool")
        nc.sync.dma_start(kw_pool[:], k_words[0].rearrange("p t b -> p (t b)").bitcast(I32))
        nc.sync.dma_start(kb_pool[0:1, :], kb[0:1, :])
        for quad in range(4):
            nc.sync.dma_start(
                ks_pool[32 * quad : 32 * quad + 4, :].bitcast(I32).rearrange("r (o c) -> r o c", o=PASSES),
                k_scales[:, 4 * quad : 4 * quad + 4, :].bitcast(I32).rearrange("o r c -> r o c"),
            )
        qw = sb.tile([P, PASSES * NQ], I32, name="qw", align_bytes=64)
        nc.sync.dma_start(
            qw[:].rearrange("p (o q) -> p o q", o=PASSES),
            q_words[0].rearrange("o p q r -> p o (q r)").bitcast(I32),
        )
        nc.sync.dma_start(vs_pool[0:1, :], vs[0:1, :])
        gate_in = sb.tile([P, HALVES, DV], F32, name="gate_in")
        nc.sync.dma_start(gate_in[:], og[0].rearrange("(h p) e -> p h e", p=P))
        v_raw = []
        for part in range(2):
            raw = sb.tile([P, 2, T // 2], F32, name="v_raw%d" % part, tag="values%d" % part)
            nc.scalar.dma_start(
                raw[:], vT.rearrange("(p h) t -> p h t", h=2)[:, :, part * T // 2 : (part + 1) * T // 2]
            )
            v_raw.append(raw)
        for quad in range(4):
            nc.gpsimd.dma_start(
                qs[32 * quad : 32 * quad + 4, :].bitcast(I32).rearrange("r (o c) -> r o c", o=PASSES),
                q_scales[0, :, 4 * quad : 4 * quad + 4, :].bitcast(I32).rearrange("o r c -> r o c"),
            )

        kw_got = sb.tile([P, N], U32, name="kw_got")
        nc.vector.tensor_copy(kw_got[:], kw_pool[:].bitcast(U32).indirect(offsets[:]))
        kb_got = sb.tile([P, N], F32, name="kb_got")
        nc.vector.tensor_copy(dealt(kb_got[:].bitcast(U32)), kb_pool[:].bitcast(U32).indirect(offsets[:]))
        ks_got = sb.tile([P, PASSES * N], U8, name="ks_got", tag="scales_then_values")
        for o in range(PASSES):
            nc.vector.tensor_copy(
                ks_got[:, o * N : (o + 1) * N], ks_pool[:, o * T : (o + 1) * T].indirect(offsets[:])
            )
        kw = []
        for pair in range(2):
            parted = sb.tile([P, PASSES * 2 * P * 2], U8, name="kw%d" % pair, align_bytes=64)
            nc.vector.tensor_copy(
                parted[:].bitcast(U16).rearrange("p (o t g i) -> p o g t i", o=PASSES, t=2, i=RUN),
                kw_got[:].bitcast(U16).rearrange("p (g t i o) -> p o g t i", o=PASSES, t=PLACES, i=RUN)[
                    :, :, :, 2 * pair : 2 * pair + 2, :
                ],
            )
            kw.append(parted)

        ks = sb.tile([P, PASSES * N], U8, name="ks", align_bytes=64)
        nc.vector.tensor_copy(
            ks[:].bitcast(I32).rearrange("p (o t g w) -> p o g t w", o=PASSES, t=PLACES, w=RUN // 4),
            ks_got[:].bitcast(I32).rearrange("p (o g t w) -> p o g t w", o=PASSES, t=PLACES, w=RUN // 4),
        )

        v_pool = sb.tile([P, 2 * T], BF16, name="v_pool")
        for part in range(2):
            nc.scalar.copy(
                v_pool[:, part * T : (part + 1) * T].rearrange("p (n h) -> p n h", h=2),
                v_raw[part][:].rearrange("p h n -> p n h"),
            )
        kb_turned = ps.tile([P, PLACES, P], F32, name="kb_turned", tag="kb_then_sum")
        for t in range(PLACES):
            nc.tensor.transpose(kb_turned[:, t, :], kb_got[:, t * P : (t + 1) * P], ident[:])
        kb_col = sb.tile([P, PLACES], F32, name="kb_col", tag="values1")
        nc.scalar.copy(kb_col[:], kb_turned[:, :, 0])

        scores = []
        for h in range(HALVES):
            for t in range(PLACES):
                if t % 2 == 0:
                    bank = ps.tile([P, PLACES, P], F32, name="scores%d%d" % (h, t // 2), tag="scores%d%d" % (h, t // 2))
                scores.append(bank[:, t % 2, :])
                for o in range(PASSES):
                    first = (o * 2 + t % 2) * 2 * P
                    q_cols = slice(o * NQ + h * P, o * NQ + (h + 1) * P)
                    nc.tensor.matmul_mx(
                        out=bank[:, t % 2, :],
                        lhsT=kw[t // 2][:, first : first + 2 * P].bitcast(FP4X4),
                        lhsT_scale=ks[:, o * N + t * P : o * N + (t + 1) * P],
                        rhs=qw[:, q_cols].bitcast(FP8X4),
                        rhs_scale=qs[:, q_cols],
                        start=(o == 0),
                        stop=(o == PASSES - 1),
                    )

        vs_got = sb.tile([P, N], F32, name="vs_got")
        nc.vector.tensor_copy(dealt(vs_got[:].bitcast(U32)), vs_pool[:].bitcast(U32).indirect(offsets[:]))
        v_got = sb.tile([P, N], F32, name="v_got", tag="scales_then_values")
        nc.vector.tensor_copy(dealt(v_got[:].bitcast(U32)), v_pool[:].bitcast(U32).indirect(offsets[:]))
        weights = []
        for h in range(HALVES):
            r = sb.tile([P, PLACES, P], F32, name="r%d" % h)
            for t in range(PLACES):
                nc.scalar.activation(r[:, t, :], scores[h * PLACES + t], ACT.Relu, bias=kb_col[:, t : t + 1])
            p = sb.tile([P, PLACES, P], F32, name="p%d" % h)
            nc.scalar.activation(p[:], r[:], ACT.Square)
            weights.append(p)

        vs_turned = ps.tile([P, PLACES, P], F32, name="vs_turned", tag="scores00")
        for t in range(PLACES):
            nc.tensor.transpose(vs_turned[:, t, :], vs_got[:, t * P : (t + 1) * P], ident[:])
        v_turned = ps.tile([P, PLACES, P], F32, name="v_turned", tag="scores10")
        for t in range(PLACES):
            nc.tensor.transpose(v_turned[:, t, :], v_got[:, t * P : (t + 1) * P], ident[:])

        v_woven = sb.tile([P, DV * PLACES], BF16, name="v_woven", align_bytes=64)
        nc.scalar.copy(
            v_woven[:].rearrange("p (e t) -> p e t", t=PLACES),
            v_turned[:].bitcast(BF16).rearrange("p t e -> p e t"),
        )
        gate = sb.tile([P, HALVES, DV], F32, name="gate")
        nc.scalar.activation(gate[:], gate_in[:], ACT.Sigmoid)

        v_codes = sb.tile([P, DV], U32, name="v_codes", align_bytes=64)
        v_scales = sb.tile([P, DV], U8, name="v_scales", align_bytes=64)
        w_woven = []
        for h in range(HALVES):
            woven = sb.tile([P, P * PLACES], BF16, name="w_woven%d" % h, align_bytes=64)
            nc.vector.tensor_tensor(
                woven[:].rearrange("p (c i t) -> p c t i", t=PLACES, i=4),
                weights[h][:].rearrange("p t (c i) -> p c t i", i=4),
                vs_turned[:, :, 0:1].unsqueeze(1).to_broadcast([P, P // 4, PLACES, 4]),
                ALU.mult,
            )
            w_woven.append(woven)
        nc.vector.quantize_mx(out=v_codes[:].bitcast(FP8X4), scales=v_scales[:], in_=v_woven[:])

        for h in range(HALVES):
            w_codes = sb.tile([P, P], U32, name="w_codes%d" % h, align_bytes=64)
            w_scales = sb.tile([P, P], U8, name="w_scales%d" % h, align_bytes=64)
            nc.vector.quantize_mx(out=w_codes[:].bitcast(FP8X4), scales=w_scales[:], in_=w_woven[h][:])

            p_sum = ps.tile([P, PLACES, P], F32, name="p_sum%d" % h, tag=("p_sum", "kb_then_sum")[h])
            for t in range(PLACES):
                nc.tensor.matmul(
                    p_sum[:, 0, :], weights[h][:, t, :], ident[:], is_transpose=True, start=(t == 0), stop=(t == PLACES - 1)
                )
            terms = sb.tile([P, P], F32, name="terms%d" % h)
            total = sb.tile([P, 1], F32, name="total%d" % h)
            nc.scalar.activation(terms[:], p_sum[:, 0, :], ACT.Identity, bias=1.0 / P, accum_out=total[:])
            inverse = sb.tile([P, 1], F32, name="inverse%d" % h)
            nc.vector.reciprocal(inverse[:], total[:])

            y = ps.tile([P, DV], F32, name="y%d" % h)
            nc.tensor.matmul_mx(
                out=y[:],
                lhsT=w_codes[:].bitcast(FP8X4),
                lhsT_scale=w_scales[:],
                rhs=v_codes[:].bitcast(FP8X4),
                rhs_scale=v_scales[:],
                start=True,
                stop=True,
            )
            result = sb.tile([P, DV], F32, name="result%d" % h)
            nc.vector.scalar_tensor_tensor(result[:], y[:], inverse[:], gate[:, h, :], ALU.mult, ALU.mult)
            nc.sync.dma_start(out[0, h * P : (h + 1) * P, :], result[:])
